import numpy as np, ml_dtypes
CORES = [8,11,14,16,19,22,24,27,30]
N = 9
TK = 32
def setup_inputs(rng):
    return {"c": rng.standard_normal((N, 128, 128), dtype=np.float32).astype(ml_dtypes.bfloat16), "x": rng.standard_normal((N, 128, TK), dtype=np.float32).astype(ml_dtypes.bfloat16)}
def setup_inputs_big(rng):
    d = setup_inputs(rng)
    for k in ("c", "x"): d[k] = (d[k].astype(np.float32) * 1024.0).astype(d[k].dtype)
    return d
def setup_inputs_small(rng):
    d = setup_inputs(rng)
    for k in ("c", "x"): d[k] = (d[k].astype(np.float32) * (1 / 1024.0)).astype(d[k].dtype)
    return d
def setup_inputs_apart(rng):
    d = setup_inputs(rng)
    f = (10.0 ** rng.permutation(np.linspace(-1.5, 1.5, N))).astype(np.float32).reshape(N, 1, 1)
    for k in ("c", "x"): d[k] = (d[k].astype(np.float32) * f).astype(d[k].dtype)
    return d
def reference(c, x):
    C, X = c.astype(np.float64), x.astype(np.float64)
    y = np.zeros((N, 128, TK))
    for r in range(N):
        for j in range(N):
            y[r] += C[(r - j) % N].T @ X[j]
    return {"y": y.astype(ml_dtypes.bfloat16 if x.dtype != np.float64 else np.float64)}

@@ -1,0 +1,158 @@
+from concourse.bass import DstId, RemoteDMATransfer
+
+N = 9
+CW = 128
+XW = 32
+W = CW + XW
+ENGINES = 8
+
+SCRATCH = {
+    "pack": ("sbuf", [128, N * W], "bfloat16"),
+    "acc": ("psum", [128, XW], "float32"),
+    "res": ("sbuf", [128, XW], "bfloat16"),
+}
+SEMAPHORES = ["loaded", "blk0", "blk1", "blk2", "sent", "mm", "rounded", "stored"]
+
+
+def _route(topo, s, d):
+    a, b, die = topo.chip(s), topo.chip(d), topo.die(s)
+    if topo.same_plane(a, b):
+        return [("out", a, die), ("in", b, die)]
+    if topo.mates(a, b):
+        return [("mate", a, die)]
+    m = [h for h in range(topo.CHIPS) if topo.mates(a, h)][0]
+    return [("mate", a, die), ("out", m, die), ("in", b, die)]
+
+
+def _plan(cores, topo):
+    chips = sorted(set(topo.chip(c) for c in cores))
+    members = dict((a, [c for c in cores if topo.chip(c) == a]) for a in chips)
+    carrier = {}
+
+    def cost():
+        load, link, cross = {}, {}, 0
+        for (a, d), s in carrier.items():
+            load[s] = load.get(s, 0) + 1
+            if topo.die(s) != topo.die(d):
+                cross += 1
+            for l in _route(topo, s, d):
+                link[l] = link.get(l, 0) + 1
+        return (max(load.values()), sum(v * v for v in load.values()), sum(v * v for v in link.values()), cross)
+
+    for sweep in range(2):
+        for a in chips:
+            dests = [d for d in cores if topo.chip(d) != a]
+            opts = [[s for s in members[a] if topo.may_write(s, d)] for d in dests]
+            total = 1
+            for o in opts:
+                total *= len(o)
+            best = None
+            for n in range(total):
+                pick = []
+                for o in opts:
+                    pick.append(o[n % len(o)])
+                    n //= len(o)
+                for d, s in zip(dests, pick):
+                    carrier[(a, d)] = s
+                k = cost()
+                if best is None or k < best[0]:
+                    best = (k, pick)
+            for d, s in zip(dests, best[1]):
+                carrier[(a, d)] = s
+    return chips, members, carrier
+
+
+def _engines(mask, n):
+    out, bit = 0, 1
+    while n and bit <= mask:
+        if mask & bit:
+            out |= bit
+            n -= 1
+        bit <<= 1
+    return out
+
+
+def rank_program(g, core, T, topo):
+    rank = T.rank_of(core)
+    if rank is None:
+        return
+    cores = list(T.cores)
+    chips, members, carrier = _plan(cores, topo)
+    mine = topo.chip(core)
+
+    order = [c for a in chips for c in members[a]]
+    slot = dict((c, i) for i, c in enumerate(order))
+
+    def cols(first, count):
+        return T.pack[:, first * W:(first + count) * W]
+
+    def block(a):
+        return cols(slot[members[a][0]], len(members[a]))
+
+    def blk(a):
+        return T.sem["blk%d" % chips.index(a)]
+
+    near = [d for d in members[mine] if d != core]
+    far = [d for d in cores if topo.chip(d) != mine and carrier[(mine, d)] == core]
+    mask = topo.mask(core, near[0])
+    for d in cores:
+        if d != core:
+            mask &= topo.mask(core, d)
+    mask = _engines(mask, ENGINES)
+
+    def send(ap, dests):
+        ids = []
+        for d in dests:
+            rid, pid, _ = topo.addr(d)
+            ids.append(DstId(rid=rid, pnc=pid))
+        g.remote_dma_fused(
+            [RemoteDMATransfer(dst_ids=ids, dma_engine_mask=mask, remote_sem=blk(mine),
+                               srcs=[ap], dsts=[ap for d in dests], alu_op=0)],
+            local_sem=T.sem.sent)
+
+    s0 = slot[core] * W
+    g.sync.dma_start(T.pack[:, s0:s0 + CW], T.c[:, :]).then_inc(T.sem.loaded, 16)
+    g.scalar.dma_start(T.pack[:, s0 + CW:s0 + W], T.x[:, :]).then_inc(T.sem.loaded, 16)
+
+    g.wait_ge(T.sem.loaded, 32)
+    send(cols(slot[core], 1), near)
+    calls = 1
+    g.wait_ge(blk(mine), ENGINES * len(near))
+    if far:
+        send(block(mine), far)
+        calls += 1
+    g.wait_ge(T.sem.sent, ENGINES * calls)
+
+    def load_of(a):
+        s = carrier[(a, core)]
+        return len([1 for v in carrier.values() if v == s])
+
+    others = sorted([a for a in chips if a != mine], key=load_of)
+    stage = {mine: 0}
+    for i, a in enumerate(others):
+        stage[a] = i + 1
+    terms = []
+    for k in range(N):
+        j = (rank - k) % N
+        terms.append((max(stage[topo.chip(cores[k])], stage[topo.chip(cores[j])]), k, j))
+    terms.sort()
+    g.tensor.wait_ge(T.sem.loaded, 32)
+    g.tensor.wait_ge(blk(mine), ENGINES * len(near))
+    reached = 0
+    for i, (st, k, j) in enumerate(terms):
+        while reached < st:
+            g.tensor.wait_ge(blk(others[reached]), ENGINES)
+            reached += 1
+        ck = slot[cores[k]] * W
+        xj = slot[cores[j]] * W + CW
+        g.tensor.matmul(T.acc[:, :], T.pack[:, ck:ck + CW], T.pack[:, xj:xj + XW],
+                        start=(i == 0), stop=(i == N - 1)).then_inc(T.sem.mm, 1)
+    while reached < len(others):
+        g.tensor.wait_ge(blk(others[reached]), ENGINES)
+        reached += 1
+
+    g.vector.wait_ge(T.sem.mm, N)
+    g.vector.tensor_copy(T.res[:, :], T.acc[:, :]).then_inc(T.sem.rounded, 1)
+    g.sync.wait_ge(T.sem.rounded, 1)
+    g.sync.dma_start(T.y[:, :], T.res[:, :]).then_inc(T.sem.stored, 16)
+    g.sync.wait_ge(T.sem.stored, 16)

@@ -11,7 +11,7 @@ SCRATCH = {
     "acc": ("psum", [128, XW], "float32"),
     "res": ("sbuf", [128, XW], "bfloat16"),
 }
-SEMAPHORES = ["loaded", "blk0", "blk1", "blk2", "sent", "mm", "rounded", "stored"]
+SEMAPHORES = ["loaded", "blk0", "blk1", "blk2", "pre0", "pre1", "pre2", "sent", "mm", "rounded", "stored"]
 
 
 def _route(topo, s, d):
@@ -80,17 +80,34 @@ def rank_program(g, core, T, topo):
     chips, members, carrier = _plan(cores, topo)
     mine = topo.chip(core)
 
-    order = [c for a in chips for c in members[a]]
+    def load_of(s):
+        return len([1 for v in carrier.values() if v == s])
+
+    seat = {}
+    for a in chips:
+        m = sorted(members[a], key=lambda c: -load_of(c))
+        seat[a] = m[:1] + m[2:] + m[1:2]
+    order = [c for a in chips for c in seat[a]]
     slot = dict((c, i) for i, c in enumerate(order))
 
     def cols(first, count):
         return T.pack[:, first * W:(first + count) * W]
 
-    def block(a):
-        return cols(slot[members[a][0]], len(members[a]))
+    def ahead(s):
+        m = seat[topo.chip(s)]
+        return len(m) > 1 and s in (m[0], m[-1])
+
+    def late(s):
+        m = seat[topo.chip(s)]
+        if not ahead(s):
+            return cols(slot[m[0]], len(m))
+        return cols(slot[m[1] if s == m[0] else m[0]], len(m) - 1)
 
     def blk(a):
         return T.sem["blk%d" % chips.index(a)]
+
+    def pre(a):
+        return T.sem["pre%d" % chips.index(a)]
 
     near = [d for d in members[mine] if d != core]
     far = [d for d in cores if topo.chip(d) != mine and carrier[(mine, d)] == core]
@@ -100,13 +117,13 @@ def rank_program(g, core, T, topo):
             mask &= topo.mask(core, d)
     mask = _engines(mask, ENGINES)
 
-    def send(ap, dests):
+    def send(ap, dests, sem):
         ids = []
         for d in dests:
             rid, pid, _ = topo.addr(d)
             ids.append(DstId(rid=rid, pnc=pid))
         g.remote_dma_fused(
-            [RemoteDMATransfer(dst_ids=ids, dma_engine_mask=mask, remote_sem=blk(mine),
+            [RemoteDMATransfer(dst_ids=ids, dma_engine_mask=mask, remote_sem=sem,
                                srcs=[ap], dsts=[ap for d in dests], alu_op=0)],
             local_sem=T.sem.sent)
 
@@ -115,40 +132,42 @@ def rank_program(g, core, T, topo):
     g.scalar.dma_start(T.pack[:, s0 + CW:s0 + W], T.x[:, :]).then_inc(T.sem.loaded, 16)
 
     g.wait_ge(T.sem.loaded, 32)
-    send(cols(slot[core], 1), near)
+    send(cols(slot[core], 1), near, blk(mine))
     calls = 1
+    if far and ahead(core):
+        send(cols(slot[core], 1), far, pre(mine))
+        calls += 1
     g.wait_ge(blk(mine), ENGINES * len(near))
     if far:
-        send(block(mine), far)
+        send(late(core), far, blk(mine))
         calls += 1
     g.wait_ge(T.sem.sent, ENGINES * calls)
 
-    def load_of(a):
+    others = sorted([a for a in chips if a != mine], key=lambda a: load_of(carrier[(a, core)]))
+    events = [pre(a) for a in others if ahead(carrier[(a, core)])] + [blk(a) for a in others]
+    stage = dict((c, 0) for c in members[mine])
+    for a in others:
         s = carrier[(a, core)]
-        return len([1 for v in carrier.values() if v == s])
-
-    others = sorted([a for a in chips if a != mine], key=load_of)
-    stage = {mine: 0}
-    for i, a in enumerate(others):
-        stage[a] = i + 1
+        for c in members[a]:
+            stage[c] = 1 + events.index(pre(a) if ahead(s) and c == s else blk(a))
     terms = []
     for k in range(N):
         j = (rank - k) % N
-        terms.append((max(stage[topo.chip(cores[k])], stage[topo.chip(cores[j])]), k, j))
+        terms.append((max(stage[cores[k]], stage[cores[j]]), k, j))
     terms.sort()
     g.tensor.wait_ge(T.sem.loaded, 32)
     g.tensor.wait_ge(blk(mine), ENGINES * len(near))
     reached = 0
     for i, (st, k, j) in enumerate(terms):
         while reached < st:
-            g.tensor.wait_ge(blk(others[reached]), ENGINES)
+            g.tensor.wait_ge(events[reached], ENGINES)
             reached += 1
         ck = slot[cores[k]] * W
         xj = slot[cores[j]] * W + CW
         g.tensor.matmul(T.acc[:, :], T.pack[:, ck:ck + CW], T.pack[:, xj:xj + XW],
                         start=(i == 0), stop=(i == N - 1)).then_inc(T.sem.mm, 1)
-    while reached < len(others):
-        g.tensor.wait_ge(blk(others[reached]), ENGINES)
+    while reached < len(events):
+        g.tensor.wait_ge(events[reached], ENGINES)
         reached += 1
 
     g.vector.wait_ge(T.sem.mm, N)

@@ -11,63 +11,36 @@ SCRATCH = {
     "acc": ("psum", [128, XW], "float32"),
     "res": ("sbuf", [128, XW], "bfloat16"),
 }
-SEMAPHORES = ["loaded", "blk0", "blk1", "blk2", "pre0", "pre1", "pre2", "sent", "mm", "rounded", "stored"]
-
-
-def _route(topo, s, d):
-    a, b, die = topo.chip(s), topo.chip(d), topo.die(s)
-    if topo.same_plane(a, b):
-        return [("out", a, die), ("in", b, die)]
-    if topo.mates(a, b):
-        return [("mate", a, die)]
-    m = [h for h in range(topo.CHIPS) if topo.mates(a, h)][0]
-    return [("mate", a, die), ("out", m, die), ("in", b, die)]
+SEMAPHORES = ["loaded", "nr", "en", "fa", "rl", "fw", "sent", "mm", "rounded", "stored"]
 
 
 def _plan(cores, topo):
     chips = sorted(set(topo.chip(c) for c in cores))
     members = dict((a, [c for c in cores if topo.chip(c) == a]) for a in chips)
-    carrier = {}
-
-    def cost():
-        load, link, cross = {}, {}, 0
-        for (a, d), s in carrier.items():
-            load[s] = load.get(s, 0) + 1
-            if topo.die(s) != topo.die(d):
-                cross += 1
-            for l in _route(topo, s, d):
-                link[l] = link.get(l, 0) + 1
-        return (max(load.values()), sum(v * v for v in load.values()), sum(v * v for v in link.values()), cross)
-
-    for sweep in range(2):
-        for a in chips:
-            dests = [d for d in cores if topo.chip(d) != a]
-            opts = [[s for s in members[a] if topo.may_write(s, d)] for d in dests]
-            total = 1
-            for o in opts:
-                total *= len(o)
-            best = None
-            for n in range(total):
-                pick = []
-                for o in opts:
-                    pick.append(o[n % len(o)])
-                    n //= len(o)
-                for d, s in zip(dests, pick):
-                    carrier[(a, d)] = s
-                k = cost()
-                if best is None or k < best[0]:
-                    best = (k, pick)
-            for d, s in zip(dests, best[1]):
-                carrier[(a, d)] = s
-    return chips, members, carrier
+    relay, entry = {}, {}
+    work = dict((c, 0) for c in cores)
+    for s in cores:
+        for d in cores:
+            if topo.chip(d) != topo.chip(s) and not topo.may_write(s, d):
+                opts = [n for n in members[topo.chip(s)] if n != s and topo.may_write(n, d)]
+                n = min(opts, key=lambda n: (work[n], topo.die(n) != topo.die(d)))
+                relay[(s, d)] = n
+                work[n] += 1
+    weak = set(s for s, d in relay)
+    for a in chips:
+        for s in cores:
+            if topo.chip(s) != a and s not in weak:
+                e = min(members[a], key=lambda e: (work[e], topo.die(e) != topo.die(s)))
+                entry[(s, a)] = e
+                work[e] += len(members[a]) - 1
+    return chips, members, relay, entry, weak
 
 
-def _engines(mask, n):
-    out, bit = 0, 1
-    while n and bit <= mask:
+def _bits(mask):
+    out, bit = [], 1
+    while bit <= mask:
         if mask & bit:
-            out |= bit
-            n -= 1
+            out.append(bit)
         bit <<= 1
     return out
 
@@ -77,98 +50,113 @@ def rank_program(g, core, T, topo):
     if rank is None:
         return
     cores = list(T.cores)
-    chips, members, carrier = _plan(cores, topo)
+    chips, members, relay, entry, weak = _plan(cores, topo)
     mine = topo.chip(core)
-
-    def load_of(s):
-        return len([1 for v in carrier.values() if v == s])
-
-    seat = {}
-    for a in chips:
-        m = sorted(members[a], key=lambda c: -load_of(c))
-        seat[a] = m[:1] + m[2:] + m[1:2]
-    order = [c for a in chips for c in seat[a]]
+    order = [c for a in chips for c in members[a]]
     slot = dict((c, i) for i, c in enumerate(order))
 
-    def cols(first, count):
-        return T.pack[:, first * W:(first + count) * W]
+    def cols(c):
+        return T.pack[:, slot[c] * W:(slot[c] + 1) * W]
 
-    def ahead(s):
-        m = seat[topo.chip(s)]
-        return len(m) > 1 and s in (m[0], m[-1])
-
-    def late(s):
-        m = seat[topo.chip(s)]
-        if not ahead(s):
-            return cols(slot[m[0]], len(m))
-        return cols(slot[m[1] if s == m[0] else m[0]], len(m) - 1)
-
-    def blk(a):
-        return T.sem["blk%d" % chips.index(a)]
-
-    def pre(a):
-        return T.sem["pre%d" % chips.index(a)]
+    def spread(e):
+        rest, calls = [s for s in cores if entry.get((s, topo.chip(e))) == e], []
+        while rest:
+            take, rest = rest[:2], rest[2:]
+            calls.append([(s, ENGINES // len(take)) for s in take])
+        return calls
 
     near = [d for d in members[mine] if d != core]
-    far = [d for d in cores if topo.chip(d) != mine and carrier[(mine, d)] == core]
     mask = topo.mask(core, near[0])
     for d in cores:
         if d != core:
             mask &= topo.mask(core, d)
-    mask = _engines(mask, ENGINES)
+    eng = _bits(mask)[:ENGINES]
+    spare = _bits(topo.mask(core, near[0]) & ~sum(eng))[:ENGINES]
+    if len(spare) < ENGINES:
+        spare = eng
+    sent = [0]
 
-    def send(ap, dests, sem):
+    def transfer(c, dests, sem, engines):
         ids = []
         for d in dests:
             rid, pid, _ = topo.addr(d)
             ids.append(DstId(rid=rid, pnc=pid))
-        g.remote_dma_fused(
-            [RemoteDMATransfer(dst_ids=ids, dma_engine_mask=mask, remote_sem=sem,
-                               srcs=[ap], dsts=[ap for d in dests], alu_op=0)],
-            local_sem=T.sem.sent)
+        sent[0] += len(engines)
+        return RemoteDMATransfer(dst_ids=ids, dma_engine_mask=sum(engines), remote_sem=sem,
+                                 srcs=[cols(c)], dsts=[cols(c) for d in dests], alu_op=0)
+
+    def send(c, dests, sem, engines):
+        g.remote_dma_fused([transfer(c, dests, sem, engines)], local_sem=T.sem.sent)
 
     s0 = slot[core] * W
     g.sync.dma_start(T.pack[:, s0:s0 + CW], T.c[:, :]).then_inc(T.sem.loaded, 16)
     g.scalar.dma_start(T.pack[:, s0 + CW:s0 + W], T.x[:, :]).then_inc(T.sem.loaded, 16)
 
+    if core in weak:
+        across = [d for d in cores if topo.chip(d) != mine and topo.may_write(core, d)]
+    else:
+        across = [entry[(core, a)] for a in chips if a != mine]
     g.wait_ge(T.sem.loaded, 32)
-    send(cols(slot[core], 1), near, blk(mine))
-    calls = 1
-    if far and ahead(core):
-        send(cols(slot[core], 1), far, pre(mine))
-        calls += 1
-    g.wait_ge(blk(mine), ENGINES * len(near))
-    if far:
-        send(late(core), far, blk(mine))
-        calls += 1
-    g.wait_ge(T.sem.sent, ENGINES * calls)
+    if core in weak:
+        send(core, near, T.sem.nr, spare)
+        if across:
+            send(core, across, T.sem.fa, eng)
+    else:
+        send(core, across, T.sem.en, eng)
+        send(core, near, T.sem.nr, spare)
 
-    others = sorted([a for a in chips if a != mine], key=lambda a: load_of(carrier[(a, core)]))
-    events = [pre(a) for a in others if ahead(carrier[(a, core)])] + [blk(a) for a in others]
-    stage = dict((c, 0) for c in members[mine])
-    for a in others:
-        s = carrier[(a, core)]
-        for c in members[a]:
-            stage[c] = 1 + events.index(pre(a) if ahead(s) and c == s else blk(a))
+    for s in near:
+        dests = [d for d in cores if relay.get((s, d)) == core]
+        if dests:
+            g.wait_ge(T.sem.nr, ENGINES * len(near))
+            send(s, dests, T.sem.rl, eng)
+    n_en = len([s for s in cores if entry.get((s, mine)) == core])
+    if n_en:
+        g.wait_ge(T.sem.en, ENGINES * n_en)
+        for call in spread(core):
+            trs, first = [], 0
+            for s, n in call:
+                trs.append(transfer(s, near, T.sem.fw, spare[first:first + n]))
+                first += n
+            g.remote_dma_fused(trs, local_sem=T.sem.sent)
+    g.wait_ge(T.sem.sent, sent[0])
+
+    events = [(T.sem.nr, ENGINES * len(near)), (T.sem.en, ENGINES * n_en),
+              (T.sem.fa, ENGINES * len([s for s in weak if topo.chip(s) != mine and topo.may_write(s, core)])),
+              (T.sem.rl, ENGINES * len([s for s in cores if (s, core) in relay])),
+              (T.sem.fw, sum(n for e in near for call in spread(e) for s, n in call))]
+    stage = {}
+    for s in cores:
+        if topo.chip(s) == mine:
+            stage[s] = 0
+        elif entry.get((s, mine)) == core:
+            stage[s] = 1
+        elif (s, core) in relay:
+            stage[s] = 3
+        elif s in weak:
+            stage[s] = 2
+        else:
+            stage[s] = 4
     terms = []
     for k in range(N):
         j = (rank - k) % N
         terms.append((max(stage[cores[k]], stage[cores[j]]), k, j))
     terms.sort()
     g.tensor.wait_ge(T.sem.loaded, 32)
-    g.tensor.wait_ge(blk(mine), ENGINES * len(near))
-    reached = 0
+    reached = -1
     for i, (st, k, j) in enumerate(terms):
         while reached < st:
-            g.tensor.wait_ge(events[reached], ENGINES)
             reached += 1
+            if events[reached][1]:
+                g.tensor.wait_ge(events[reached][0], events[reached][1])
         ck = slot[cores[k]] * W
         xj = slot[cores[j]] * W + CW
         g.tensor.matmul(T.acc[:, :], T.pack[:, ck:ck + CW], T.pack[:, xj:xj + XW],
                         start=(i == 0), stop=(i == N - 1)).then_inc(T.sem.mm, 1)
-    while reached < len(events):
-        g.tensor.wait_ge(events[reached], ENGINES)
+    while reached < len(events) - 1:
         reached += 1
+        if events[reached][1]:
+            g.tensor.wait_ge(events[reached][0], events[reached][1])
 
     g.vector.wait_ge(T.sem.mm, N)
     g.vector.tensor_copy(T.res[:, :], T.acc[:, :]).then_inc(T.sem.rounded, 1)

from concourse.bass import DstId, RemoteDMATransfer

N = 9
CW = 128
XW = 32
W = CW + XW
ENGINES = 8

SCRATCH = {
    "pack": ("sbuf", [128, N * W], "bfloat16"),
    "acc": ("psum", [128, XW], "float32"),
    "res": ("sbuf", [128, XW], "bfloat16"),
}
SEMAPHORES = ["loaded", "nr", "en", "fa", "rl", "fw", "sent", "mm", "rounded", "stored"]


def _plan(cores, topo):
    chips = sorted(set(topo.chip(c) for c in cores))
    members = dict((a, [c for c in cores if topo.chip(c) == a]) for a in chips)
    relay, entry = {}, {}
    work = dict((c, 0) for c in cores)
    for s in cores:
        for d in cores:
            if topo.chip(d) != topo.chip(s) and not topo.may_write(s, d):
                opts = [n for n in members[topo.chip(s)] if n != s and topo.may_write(n, d)]
                n = min(opts, key=lambda n: (work[n], topo.die(n) != topo.die(d)))
                relay[(s, d)] = n
                work[n] += 1
    weak = set(s for s, d in relay)
    for a in chips:
        for s in cores:
            if topo.chip(s) != a and s not in weak:
                e = min(members[a], key=lambda e: (work[e], topo.die(e) != topo.die(s)))
                entry[(s, a)] = e
                work[e] += len(members[a]) - 1
    return chips, members, relay, entry, weak


def _bits(mask):
    out, bit = [], 1
    while bit <= mask:
        if mask & bit:
            out.append(bit)
        bit <<= 1
    return out


def rank_program(g, core, T, topo):
    rank = T.rank_of(core)
    if rank is None:
        return
    cores = list(T.cores)
    chips, members, relay, entry, weak = _plan(cores, topo)
    mine = topo.chip(core)
    order = [c for a in chips for c in members[a]]
    slot = dict((c, i) for i, c in enumerate(order))

    def cols(c):
        return T.pack[:, slot[c] * W:(slot[c] + 1) * W]

    def spread(e):
        rest, calls = [s for s in cores if entry.get((s, topo.chip(e))) == e], []
        while rest:
            take, rest = rest[:2], rest[2:]
            calls.append([(s, ENGINES // len(take)) for s in take])
        return calls

    near = [d for d in members[mine] if d != core]
    mask = topo.mask(core, near[0])
    for d in cores:
        if d != core:
            mask &= topo.mask(core, d)
    eng = _bits(mask)[:ENGINES]
    spare = _bits(topo.mask(core, near[0]) & ~sum(eng))[:ENGINES]
    if len(spare) < ENGINES:
        spare = eng
    sent = [0]

    def transfer(c, dests, sem, engines):
        ids = []
        for d in dests:
            rid, pid, _ = topo.addr(d)
            ids.append(DstId(rid=rid, pnc=pid))
        sent[0] += len(engines)
        return RemoteDMATransfer(dst_ids=ids, dma_engine_mask=sum(engines), remote_sem=sem,
                                 srcs=[cols(c)], dsts=[cols(c) for d in dests], alu_op=0)

    def send(c, dests, sem, engines):
        g.remote_dma_fused([transfer(c, dests, sem, engines)], local_sem=T.sem.sent)

    s0 = slot[core] * W
    g.sync.dma_start(T.pack[:, s0:s0 + CW], T.c[:, :]).then_inc(T.sem.loaded, 16)
    g.scalar.dma_start(T.pack[:, s0 + CW:s0 + W], T.x[:, :]).then_inc(T.sem.loaded, 16)

    if core in weak:
        across = [d for d in cores if topo.chip(d) != mine and topo.may_write(core, d)]
    else:
        across = [entry[(core, a)] for a in chips if a != mine]
    g.wait_ge(T.sem.loaded, 32)
    if core in weak:
        send(core, near, T.sem.nr, spare)
        if across:
            send(core, across, T.sem.fa, eng)
    else:
        send(core, across, T.sem.en, eng)
        send(core, near, T.sem.nr, spare)

    for s in near:
        dests = [d for d in cores if relay.get((s, d)) == core]
        if dests:
            g.wait_ge(T.sem.nr, ENGINES * len(near))
            send(s, dests, T.sem.rl, eng)
    n_en = len([s for s in cores if entry.get((s, mine)) == core])
    if n_en:
        g.wait_ge(T.sem.en, ENGINES * n_en)
        for call in spread(core):
            trs, first = [], 0
            for s, n in call:
                trs.append(transfer(s, near, T.sem.fw, spare[first:first + n]))
                first += n
            g.remote_dma_fused(trs, local_sem=T.sem.sent)
    g.wait_ge(T.sem.sent, sent[0])

    events = [(T.sem.nr, ENGINES * len(near)), (T.sem.en, ENGINES * n_en),
              (T.sem.fa, ENGINES * len([s for s in weak if topo.chip(s) != mine and topo.may_write(s, core)])),
              (T.sem.rl, ENGINES * len([s for s in cores if (s, core) in relay])),
              (T.sem.fw, sum(n for e in near for call in spread(e) for s, n in call))]
    stage = {}
    for s in cores:
        if topo.chip(s) == mine:
            stage[s] = 0
        elif entry.get((s, mine)) == core:
            stage[s] = 1
        elif (s, core) in relay:
            stage[s] = 3
        elif s in weak:
            stage[s] = 2
        else:
            stage[s] = 4
    terms = []
    for k in range(N):
        j = (rank - k) % N
        terms.append((max(stage[cores[k]], stage[cores[j]]), k, j))
    terms.sort()
    g.tensor.wait_ge(T.sem.loaded, 32)
    reached = -1
    for i, (st, k, j) in enumerate(terms):
        while reached < st:
            reached += 1
            if events[reached][1]:
                g.tensor.wait_ge(events[reached][0], events[reached][1])
        ck = slot[cores[k]] * W
        xj = slot[cores[j]] * W + CW
        g.tensor.matmul(T.acc[:, :], T.pack[:, ck:ck + CW], T.pack[:, xj:xj + XW],
                        start=(i == 0), stop=(i == N - 1)).then_inc(T.sem.mm, 1)
    while reached < len(events) - 1:
        reached += 1
        if events[reached][1]:
            g.tensor.wait_ge(events[reached][0], events[reached][1])

    g.vector.wait_ge(T.sem.mm, N)
    g.vector.tensor_copy(T.res[:, :], T.acc[:, :]).then_inc(T.sem.rounded, 1)
    g.sync.wait_ge(T.sem.rounded, 1)
    g.sync.dma_start(T.y[:, :], T.res[:, :]).then_inc(T.sem.stored, 16)
    g.sync.wait_ge(T.sem.stored, 16)
